import numpy as np, ml_dtypes
CORES = [6,15,38,47]
N = 4
BF = ml_dtypes.bfloat16
def gentries(a):
    return np.ascontiguousarray(a.reshape(8, 16, -1).transpose(0, 2, 1)).reshape(8, -1)
def gtable(e):
    e = np.asarray(e); return np.ascontiguousarray(e.reshape(8, -1, 16).transpose(0, 2, 1)).reshape(128, -1).astype(np.int32)
T, C, RO = 1024, 64, 3
M = 3 * T
S = (N - 1) * C
def glue(rng, w, free, slots):
    o = rng.permutation(free); n = len(slots); w[o[:n]] = M + slots; p = o[n:]
    if len(p) % 2:
        w[p[-1]] = p[-1]; p = p[:-1]
    w[p[0::2]] = p[1::2]; w[p[1::2]] = p[0::2]
def sends(w):
    at = np.zeros(S, np.int64); b = np.nonzero(w >= M)[0]; at[w[b] - M] = b
    return np.concatenate([at[(N - d - 1) * C:(N - d) * C] for d in range(1, N)])
def parts(rng):
    w = np.zeros((N, 8, M), np.int64); s = np.zeros((N, 8, S), np.int64)
    for q in range(N):
        for g in range(8):
            glue(rng, w[q, g], np.arange(M), rng.permutation(S)); s[q, g] = sends(w[q, g])
    amp = rng.choice(np.array([60.0, 150.0, 255.0]), (N, 8, 16, 1))
    X = np.rint(amp * (2 * rng.random((N, 8, 16, M)) - 1)).astype(np.int64)
    return X, w, s
def plant(rng, X, h, g):
    z = rng.integers(40, 251, (16, len(h))) * rng.choice(np.array([-1, 1]), (16, len(h)))
    for e, v in ((h, z), (g, -z)):
        X[:, e] = v; X[:, (e + T) % M] = -v; X[:, (e + 2 * T) % M] = rng.integers(-3, 4, z.shape)
def twice(rng, X, h, g):
    z = rng.choice(np.array([-1, 1]), (16, len(h))); v = rng.integers(50, 61, z.shape)
    for e, y in ((h, z), (g, -z)):
        X[:, e] = y * rng.integers(230, 251, z.shape); X[:, (e + T) % M] = rng.integers(-3, 4, z.shape); X[:, (e + 2 * T) % M] = y * v
def rivals(rng, X, w):
    n = T // 8; k = np.arange(n); o = rng.permutation(T)[:3 * n].reshape(3, n); m = k % 3; i = np.arange(16)[:, None]
    z = rng.choice(np.array([-1, 1]), (16, n)); p = rng.integers(200, 251, (16, n)); u = rng.integers(0, 101, (16, n)); used = []
    X[:, m * T + o[0]] = -z * p; X[:, ((m + 1) % 3) * T + o[0]] = -z * p; X[:, ((m + 2) % 3) * T + o[0]] = z * rng.integers(200, 256, (16, n))
    for j, few, v in ((1, (k // 3) % 5, u), (2, (k // 15) % 5, np.concatenate([u[:4], u[:3:-1]]))):
        h = ((m + j) % 3) * T + o[0]; e = rng.integers(0, 3, n) * T + o[j]; w[h] = e; w[e] = h; used += [h, e]
        y = z * (1 - 2 * (i % 2)) * rng.integers(240, 256, (16, n))
        X[:, e] = y; X[:, (e + T) % M] = -y; X[:, (e + 2 * T) % M] = z * (np.where(i < 4, (i < few).astype(np.int64), v) - p)
    glue(rng, w, np.setdiff1d(np.arange(M), np.concatenate(used)), rng.permutation(S))
def pack(X, w, s):
    return {"x": np.ascontiguousarray(X.reshape(N, 128, M)).astype(np.float32).astype(BF), "twn": w.astype(np.int32), "snd": np.stack([gtable(a) for a in s])}
def setup_inputs(rng):
    return pack(*parts(rng))
def setup_inputs_ties(rng):
    X, w, s = parts(rng)
    for g in range(8):
        if g % 4 == 0:
            X[:, g] = rng.integers(-255, 256, (1, 16, 1)); live = rng.permutation(16)[:3]
            X[:, g, live] = rng.integers(0, 2, (N, 3, M))
        elif g % 4 == 1: X[:, g] = 255 * (2 * rng.integers(0, 2, (N, 16, M)) - 1)
        elif g % 4 == 2: X[:, g] = rng.integers(-1, 2, (N, 16, M))
        else: X[:, g] = rng.integers(-255, 256, (N, 16, 1))
    for q in range(N):
        for g in (5, 6):
            rivals(rng, X[q, g], w[q, g]); s[q, g] = sends(w[q, g])
    return pack(X, w, s)
def setup_inputs_ends(rng):
    X, w, s = parts(rng)
    for q in range(N):
        glue(rng, w[q, 0], np.arange(M), np.zeros(0, np.int64))
        w[q, 1] = M + rng.integers(0, S, M)
        o = rng.permutation(M); w[q, 2, o[:T]] = o[:T]; glue(rng, w[q, 2], o[T:], rng.permutation(S))
        t = rng.permutation(T)[:T // 4]; w[q, 3, t] = T + t; w[q, 3, T + t] = t
        glue(rng, w[q, 3], np.setdiff1d(np.arange(M), np.concatenate([t, T + t])), rng.permutation(S))
        o = rng.permutation(T).reshape(2, -1)
        for i in range(3):
            a = i * T + o[0]; b = ((3 - i) % 3) * T + o[1]; w[q, 4, a] = b; w[q, 4, b] = a
        glue(rng, w[q, 5], np.arange(M), rng.choice(np.array([0, C - 1, S - 1]), T))
        w[q, 6, 0] = M - 1; w[q, 6, M - 1] = 0; glue(rng, w[q, 6], np.arange(1, M - 1), rng.permutation(S)); plant(rng, X[q, 6], np.array([0]), np.array([M - 1]))
    s[:, 0::2] = rng.choice(np.array([0, T - 1, T, 2 * T - 1, 2 * T, M - 1]), (N, 4, S)); s[:, 1::2] = rng.integers(0, M, (N, 4, S))
    return pack(X, w, s)
def setup_inputs_whirl(rng):
    X, w, s = parts(rng)
    for q in range(N):
        for g in range(8):
            o = rng.permutation(T).reshape(2, -1); p = rng.integers(0, 3, o.shape) * T + o; h, e = p[0], p[1]
            w[q, g, h] = e; w[q, g, e] = h; rest = np.setdiff1d(np.arange(M), p.reshape(-1))
            if g in (2, 6):
                b = rng.permutation((p.reshape(-1) + T) % M)[:S]
                glue(rng, w[q, g], b, rng.permutation(S)); glue(rng, w[q, g], np.setdiff1d(rest, b), np.zeros(0, np.int64))
                twice(rng, X[q, g], h, e)
            else:
                glue(rng, w[q, g], rest, rng.permutation(S))
                n = T // 2 if g % 2 == 0 else T // 4
                plant(rng, X[q, g], h[:n], e[:n])
            s[q, g] = sends(w[q, g])
        X[q, 7] = rng.integers(-255, 256, (16, 1))
    return pack(X, w, s)
def setup_inputs_mesh(rng):
    X, w, s = parts(rng); K = T // 32; cell = np.arange(16 * K).reshape(16, K)
    left = np.roll(cell, 1, axis=1).ravel(); down = np.roll(cell, -1, axis=0); right = np.roll(cell, -1, axis=1).ravel(); far = np.roll(down, -1, axis=1).ravel()
    down = down.ravel(); row = np.repeat(np.arange(16), K); col = np.tile(np.arange(K), 16); cell = cell.ravel()
    a = 2 * cell; b = a + 1; w0 = np.zeros(M, np.int64); org = np.zeros(M, np.int64)
    w0[2 * T + a] = b; w0[b] = 2 * T + a
    bl = 2 * left + 1; w0[a] = T + bl; w0[T + bl] = a
    bd = 2 * down + 1; w0[T + a] = 2 * T + bd; w0[2 * T + bd] = T + a
    org[a] = cell; org[T + a] = down; org[2 * T + a] = far; org[b] = cell; org[T + b] = far; org[2 * T + b] = right
    low = np.nonzero(w0 > np.arange(M))[0]; tri = np.arange(M) % T; side = np.arange(M) // T
    for q in range(N):
        for g in range(8):
            place = rng.permutation(T); turn = rng.integers(0, 3, T); ren = ((side + turn[tri]) % 3) * T + place[tri]
            w[q, g, ren] = ren[w0]; c = rng.permutation(low)[:S // 2]; c = np.concatenate([c, w0[c]]); w[q, g, ren[c]] = M + rng.permutation(S)
            v = 120 * np.sin(rng.random((16, 1)) * row + rng.random((16, 1)) * col + 6 * rng.random((16, 1))) + 40 * rng.standard_normal((16, 16 * K))
            X[q, g][:, ren] = np.clip(np.rint(v), -255, 255).astype(np.int64)[:, org]; s[q, g] = sends(w[q, g])
    return pack(X, w, s)
def setup_inputs_spread(rng):
    X, w, s = parts(rng)
    X = np.exp2(8 * rng.random((N, 8, 1, M))) * (rng.random((N, 8, 1, M)) > 0.0625) * (2 * rng.random((N, 8, 16, M)) - 1)
    X = np.clip(np.rint(X), -255, 255).astype(np.int64)
    for q in range(N):
        for g in range(8):
            glue(rng, w[q, g], np.arange(M), (S * rng.random(int(rng.integers(0, T))) ** 2).astype(np.int64))
    return pack(X, w, (M * rng.random((N, 8, S)) ** 3).astype(np.int64))
def check_inputs(d):
    bad = []; v = np.asarray(d["x"]).astype(np.float32); w = np.asarray(d["twn"]).astype(np.int64)
    if not (np.all(v == np.rint(v)) and np.all(np.abs(v) <= 255)): bad.append("whole numbers of x")
    for k, hi in (("twn", M + S - 1), ("snd", M - 1)):
        if np.min(d[k]) < 0 or np.max(d[k]) > hi: bad.append("range of " + k)
    back = np.take_along_axis(w, np.clip(w, 0, M - 1), 2)
    if np.any((w < M) & (back != np.arange(M))): bad.append("twins of twins in twn")
    return bad
def reference(x, twn, snd):
    X = x.astype(np.float32).astype(np.int32).reshape(N, 8, 16, M); tw = twn.astype(np.int64)
    sl = np.stack([gentries(a) for a in snd]).astype(np.int64)
    h = np.arange(M); nx = (h + T) % M; pv = (h + 2 * T) % M
    for rnd in range(RO):
        give = np.take_along_axis(X, pv[sl][:, :, None, :], 3)
        come = np.stack([np.concatenate([give[(a - d) % N][..., (d - 1) * C:d * C] for d in range(1, N)], axis=2) for a in range(N)])
        own = tw < M; t = np.minimum(tw, M - 1)
        D = np.take_along_axis(np.concatenate([X, come], axis=3), np.where(own, pv[t], tw)[:, :, None, :], 3)
        far = X[..., pv]
        gain = np.sum((X - X[..., nx]) ** 2 - (far - D) ** 2, axis=2)
        gain = np.where(own & (t % T != h % T), gain, 0).reshape(N, 8, 3, T)
        best = np.argmax(gain, axis=2)
        took = ((np.arange(3)[:, None] == best[:, :, None, :]) & (gain > 0)).reshape(N, 8, M)
        flip = took & own & np.take_along_axis(took, t, 2)
        Y = np.where(own[:, :, None, :], far, np.maximum(far, D))[..., nx]
        fn = flip[..., pv]; fp = flip[..., nx]
        loc = np.where(fn, pv[t][..., pv], np.where(fp, pv, h)); src = np.where(fn, nx, np.where(fp, nx[t][..., nx], h))
        X = np.take_along_axis(Y, np.where(flip, pv[t], src)[:, :, None, :], 3)
        e = np.take_along_axis(tw, src, 2)
        tw = np.where(e < M, np.take_along_axis(loc, np.minimum(e, M - 1), 2), e)
        sl = np.take_along_axis(loc, sl, 2)
    return {"yx": X.reshape(N, 128, M).astype(np.float32).astype(BF), "yt": tw.astype(np.float32)}

import math
from concourse.bass import DstId, RemoteDMATransfer
from concourse.mybir import AluOpType as ALU, ActivationFunctionType as ACT

TT, M, S, RO = 1024, 3072, 192, 3
LW = 204
CW = 208
BIG = float(2 ** 23)
IDW = [1, -1, -BIG, 16, 128, 64, -64, 2048, 1024, -1024, -2048]
YCUT = ((256, 1280, 1792, 2048, 3072), (256, 1280, 1792, 2048, 3072))
MCUT = 0
TG = 384
FQ = (("S", 0, 0), ("V", 1, 0), ("S", 2, 0), ("V", 0, 1), ("V", 1, 1), ("S", 2, 1))
TQ = (("V", 0, 640), ("S", 640, 1216), ("V", 1216, 1728), ("S", 1728, 2240), ("S", 2240, M + S))
FL = (("S", 0, 0), ("V", 1, 0), ("S", 0, 1), ("V", 1, 1), ("S", 2, 0), ("S", 2, 1))
TL = (("V", 0, 1024), ("S", 1792, 2560), ("V", 1024, 1792), ("S", 2560, M))


def _sb(dt, **k):
    return {n: ("sbuf", [128, w], dt) for n, w in k.items()}


SCRATCH = {}
SCRATCH.update(_sb("bfloat16", F=M + S, F2=M, YF=M, TR=M + S, LR=M + S, CM=RO * CW, GV=RO * S, MR=TT, NR=TT, DA=192, DB=192,
                   IV=384, ST=384, SW=192, AT=64, VAL=192, PW=64, VF=256, MM=768, LA=LW, LB=LW, ID=128 * len(IDW),
                   SE=4 * 144, R4=256, TE=384, HF=64, AB=384, AC=LW, W2J=2))
SCRATCH.update(_sb("float32", V32=M, SL=M, LR32=M + S, TW32=M, SC=12, M0=128, M1=128, M2=128, PR=192, P1=64, P2=64,
                   N1=64, N2=64, X1=64, TP=LW, E1=192, E2=192, E3=192, L32=LW, CF=16, DI=128, XI=144, GI=16, RI=64,
                   TI=64, HI=128, I32=256, GS=32, TM=64, Q1=24, Q2=12, Q3=12, Q4=12, Q5=12, Q6=12, T1=384, T2=384, TW=192))
SCRATCH.update(_sb("int32", TB=192, TA=192, TC=192, SN=12, SA=12, SB=12, DD=192, AN=192, Z=64, AI=64, BI=64, X2=64,
                   PI=8, QI=12))
SCRATCH.update(_sb("uint16", EL=LW, BL=192, SR=192, EP=LW, MO=64, NG=64, L1=24, L2=12))
PSUM = ("K", "U0", "U1", "U2", "U3", "W0", "W1", "W2")
SCRATCH.update({n: ("psum", [128, 512], "float32") for n in PSUM})
NDMA = 32
SEMAPHORES = ["cV", "cS", "cP", "cG", "sent", "arr0", "arr1", "arr2"] + ["d%d" % i for i in range(NDMA)]


def build(g, core, T, topo):
    ops = []
    rank = T.rank_of(core)
    n = len(T.cores)
    LN2 = math.log(2.0)

    def A(name, lo, hi):
        return (T[name][:, lo:hi], (name, lo, hi))

    def W(name, lo, hi, off, c0, c1):
        return (T[name][:, lo:hi].indirect(T[off][:, c0:c1]), (name, lo, hi), (off, c0, c1))

    def regs(*xs):
        out = []
        for x in xs:
            if isinstance(x, tuple): out.extend(x[1:])
        return out

    def ap(x):
        return x[0] if isinstance(x, tuple) else x

    def add(q, fn, rd, wr, kind="c"):
        ops.append((q, fn, rd, wr, kind))

    def tt(o, a, b, op):
        add("V", lambda: g.vector.tensor_tensor(o[0], a[0], b[0], op), regs(a, b), regs(o))

    def ts(o, a, s1, op0, s2=None, op1=None):
        if op1 is None:
            add("V", lambda: g.vector.tensor_scalar(o[0], a[0], ap(s1), None, op0), regs(a, s1), regs(o))
        else:
            add("V", lambda: g.vector.tensor_scalar(o[0], a[0], ap(s1), ap(s2), op0, op1), regs(a, s1, s2), regs(o))

    def cp(o, a):
        add("V", lambda: g.vector.tensor_copy(o[0], a[0]), regs(a), regs(o))

    def ms(o, v):
        add("V", lambda: g.vector.memset(o[0], v), [], regs(o))

    def act(o, a, f, bias=0.0, scale=1.0):
        add("S", lambda: g.scalar.activation(o[0], a[0], f, bias=ap(bias), scale=ap(scale)), regs(a, bias, scale), regs(o))

    def gat(q, o, w):
        if q == "V": cp(o, w)
        else: add("S", lambda: g.scalar.activation(o[0], w[0], ACT.Copy), regs(w), regs(o))

    def mm(o, l, r, st, sp):
        add("P", lambda: g.tensor.matmul(o[0], l[0], r[0], st, sp), regs(l, r), regs(o))

    def iota(o, pat, base, cm, fl=True):
        if fl: add("G", lambda: g.iota(o[0], pat, base, cm, allow_small_or_imprecise_dtypes=True), [], regs(o))
        else: add("G", lambda: g.iota(o[0], pat, base, cm), [], regs(o))

    def dma(q, o, i, rd, wr):
        eng = {"Y": g.sync, "S": g.scalar}[q]
        add(q, lambda: eng.dma_start(o, i), rd, wr, "d")

    def I(w):
        k = IDW.index(w)
        return A("ID", 128 * k, 128 * k + 128)

    J, G16, EV, OD, UH, WN, WP, T0, T1, JL, W2 = [A("CF", k, k + 1) for k in range(11)]
    IP, IN = A("I32", 0, 128), A("I32", 128, 256)
    DI = A("DI", 0, 128)

    def wrap(sel, src, lo, hi, out, start=True):
        for j in range(16):
            mm(out, A("SE", 144 * sel + 15 - j, 144 * sel + 143 - j), (T[src][:, lo + j:hi:16], (src, lo, hi)), start and j == 0, j == 15)

    def hops2(a, b):
        ca, cb = topo.chip(a), topo.chip(b)
        return ca != cb and not topo.mates(ca, cb) and not topo.same_plane(ca, cb)

    def share(q):
        peers = [T.cores[(q + d) % n] for d in range(1, n)]
        far = [hops2(T.cores[q], p) for p in peers]
        big = far.index(True) if True in far else 0
        return [4 if k == big else 2 for k in range(n - 1)]
    arrive = sum(share((rank - d) % n)[d - 1] for d in range(1, n))

    def send(r):
        gat("V", A("GV", r * S, r * S + S), W("F", 0, M + S, "EL", 0, 12))
        trs = []; at = 0
        for d in range(1, n):
            dst = T.cores[(rank + d) % n]; k = share(rank)[d - 1]
            eng = topo.engines(core, dst)[at:at + k]; at += k
            rid, pid, _se = topo.addr(dst)
            trs.append(RemoteDMATransfer(dst_ids=[DstId(rid=rid, pnc=pid)], dma_engine_mask=sum(1 << e for e in eng),
                                         remote_sem=T.sem["arr%d" % r], src=T.GV[:, r * S + (d - 1) * 64:r * S + d * 64],
                                         dst=T.CM[:, r * CW + 16 + (d - 1) * 64:r * CW + 16 + d * 64]))
        add("G", lambda: g.remote_dma_fused(trs, local_sem=T.sem.sent), [("GV", r * S, r * S + S)], [], "r")
        add("X", ("arr%d" % r, arrive), [], [("CM", r * CW + 16, r * CW + CW)], "x")

    dma("Y", T.TB[:], T.twn[:], [], [("TB", 0, 192)])
    dma("S", T.SN[:], T.snd[:], [], [("SN", 0, 12)])
    dma("Y", T.F[:, 0:TT], T.x[:, 2 * TT:M], [], [("F", 0, TT)])
    dma("S", T.F[:, TT:M], T.x[:, 0:2 * TT], [], [("F", TT, M)])
    dma("Y", T.F2[:, 0:TT], T.x[:, 2 * TT:M], [], [("F2", 0, TT)])
    dma("S", T.F2[:, TT:2 * TT], T.x[:, 0:TT], [], [("F2", TT, 2 * TT)])
    iota(A("PI", 0, 1), [[0, 1]], 0, 1, False)
    iota(A("Q1", 0, 24), [[16, 12], [0, 2]], 0, 0)
    iota(A("Q2", 0, 12), [[16, 12]], 0, 0)
    iota(DI, [[1, 128]], 0, -1)
    iota(A("HI", 0, 128), [[0, 8], [1, 2], [0, 8]], 0, 0)
    iota(A("GI", 0, 16), [[16, 8], [0, 2]], 0, 0)
    iota(A("TI", 0, 64), [[16, 64]], -TT, 0)
    iota(A("XI", 0, 144), [[1, 144]], -15, 0)
    iota(A("RI", 0, 64), [[2, 64]], 0, 0)
    iota(A("AC", 0, LW), [[1, LW]], 0, 0)
    iota(A("TR", 0, TG), [[0, TG]], 0, 0)
    for k, m in enumerate((15, 112, 126, 1, 16)): ts(A("PI", k + 1, k + 2), A("PI", 0, 1), m, ALU.bitwise_and)
    cp(A("CF", 0, 5), A("PI", 1, 6))
    ts(A("L1", 0, 24), A("Q1", 0, 24), J, ALU.add)
    ts(A("Q3", 0, 12), A("Q2", 0, 12), J, ALU.add)
    ms(A("F", M, M + S), 1024.0)
    ts(A("Q4", 0, 12), A("Q3", 0, 12), -5.5, ALU.add, 1.0 / 12, ALU.mult)
    ts(A("Q5", 0, 12), A("Q3", 0, 12), 32.0, ALU.mult, UH, ALU.add)
    cp(A("QI", 0, 12), A("Q4", 0, 12))
    ts(I(1), DI, 0.0, ALU.is_equal, 1.0, ALU.mult)
    ts(A("Q6", 0, 12), A("QI", 0, 12), -383.0, ALU.mult)
    ts(I(-1), DI, 0.0, ALU.is_equal, -1.0, ALU.mult)
    tt(A("Q4", 0, 12), A("Q6", 0, 12), A("Q5", 0, 12), ALU.add)
    ts(A("M1", 0, 128), A("HI", 0, 128), OD, ALU.not_equal, -BIG, ALU.mult)
    cp(A("T1", 0, 384), W("TB", 0, 192, "L1", 0, 24))
    cp(A("L2", 0, 12), A("Q4", 0, 12))
    add("V", lambda: g.vector.transpose(T.T2[:], T.T1[:]), [("T1", 0, 384)], [("T2", 0, 384)])
    cp(A("EL", 0, 12), A("SN", 0, 12))
    cp(A("TW", 0, 192), W("T2", 0, 384, "L2", 0, 12))
    send(0)
    iota(A("TR", TG, M + S), [[0, M + S - TG]], 0, 0)
    iota(A("LR", 0, M + S), [[0, M + S]], 0, 0)
    cp(A("EL", 12, LW), A("TW", 0, 192))
    ts(A("GS", 0, 16), A("GI", 0, 16), G16, ALU.is_equal, 1.0, ALU.mult)
    act(A("W2J", 0, 1), J, ACT.Exp, 0.0, LN2)
    act(W2, A("W2J", 0, 1), ACT.Copy)
    for q in range(3): act(A("TE", 128 * q, 128 * q + 128), A("M1", 0, 128), ACT.Copy, -0.25 * (q + 1))
    act(I(-BIG), I(1), ACT.Copy, 0.0, -BIG)

    def later():
        ts(A("TA", 0, 192), A("TB", 0, 192), 4, ALU.arith_shift_right)
        ts(A("TC", 0, 192), A("TB", 0, 192), 15, ALU.bitwise_and)
        ts(T0, J, 0.0, ALU.is_equal); ts(T1, J, 1.0, ALU.is_equal)
        cp(A("DA", 0, 192), A("TA", 0, 192)); cp(A("DB", 0, 192), A("TC", 0, 192))
        dma("Y", T.TR[0:128:16, S:S + M], T.DA[:], [("DA", 0, 192)], [("TR", S, S + M - 1)])
        dma("Y", T.TR[1:128:16, S:S + M], T.DB[:], [("DB", 0, 192), ("TR", 0, 1)], [("TR", S + M - 1, S + M)])
        ts(WN, T0, 16.0, ALU.mult, T1, ALU.add); ts(WP, T1, float(LW), ALU.mult, T0, ALU.add)
        ts(JL, J, -LN2, ALU.mult, -LN2, ALU.add)
        ms(A("HF", 0, 64), 0.5)
        ts(A("R4", 0, 64), A("RI", 0, 64), EV, ALU.is_equal)
        ts(A("SE", 432, 576), A("XI", 0, 144), G16, ALU.is_equal)
        ts(A("SA", 0, 12), A("SN", 0, 12), 4, ALU.arith_shift_right)
        ts(A("SB", 0, 12), A("SN", 0, 12), 15, ALU.bitwise_and)
        ts(A("L32", 192, LW), A("AC", 192, LW), 16.0, ALU.mult, J, ALU.add)
        ts(A("SC", 0, 12), A("SB", 0, 12), float(LW), ALU.mult)
        ts(A("LB", 192, LW), A("AC", 192, LW), 0.0, ALU.mult, J, ALU.add)
        tt(A("TP", 0, 12), A("SC", 0, 12), A("SA", 0, 12), ALU.add)

    def later_s():
        for k in range(1, 4): act(A("R4", 64 * k, 64 * k + 64), A("R4", 0, 64), ACT.Copy)
        for k, w in ((1, WP), (2, W2), (0, WN)): act(A("SE", 144 * k, 144 * k + 144), A("SE", 432, 576), ACT.Identity, 0.0, w)
        for w in IDW[3:]: act(I(w), I(1), ACT.Copy, 0.0, float(w))
        act(IP, I(1), ACT.Copy); act(IN, I(-1), ACT.Copy)
        act(A("AB", 0, 192), A("AC", 0, 192), ACT.Copy)
        act(A("AB", 192, 384), A("AC", 0, 192), ACT.Identity, J, 0.0)
        act(A("LA", 192, LW), A("AC", 192, LW), ACT.Copy)

    UB = ["U0", "U1", "U2", "U3"]
    WB = ["W0", "W1", "W2"]
    UC = [(0, 0), (1, 0), (0, 1), (2, 0), (1, 1), (2, 1)]
    KS = [("K", 0), ("K", 128), ("W1", 0)]
    KR = [("K", 0, 256), ("K", 0, 256), ("W1", 0, 128)]

    def KK(p):
        return A(KS[p][0], KS[p][1], KS[p][1] + 128)

    def umm(k):
        p, hf = UC[k]; o = A(UB[k % 4], 0, 512)
        a = ((p + 1) % 3) * TT + hf * 512; b = ((p + 2) % 3) * TT + hf * 512
        mm(o, I(1), A("F", a, a + 512), True, False); mm(o, I(-1), A("F", b, b + 512), False, True)

    def sql(k):
        p, hf = UC[k]; a = p * TT + hf * 512
        act(A("SL", a, a + 512), A(UB[k % 4], 0, 512), ACT.Square)

    def ssum(src, p, sg, last=False):
        for j in range(8):
            mm((T[KS[p][0]][:, KS[p][1] + j:KS[p][1] + 128:8], KR[p]), (T[src][:, p * TT + j:(p + 1) * TT:8], (src, p * TT, (p + 1) * TT)),
               A("GS", 16 * sg, 16 * sg + 16), False, last and j == 7)

    def inv(p, last=False):
        mm((KK(p)[0], KR[p]), (T.IV[:, 128 * p:128 * p + 128], ("IV", 0, 384)), I(-BIG), False, last)

    def ystep(r, k):
        lo, hi = (0 if k == 0 else YCUT[r > 0][k - 1]), YCUT[r > 0][k]
        if hi > lo: tt(A("YF", lo, hi), W("CM", r * CW, r * CW + CW, "BL", lo // 16, hi // 16), A("F", lo, hi), ALU.max)

    for r in range(RO):
        last = r == RO - 1
        c0 = 12 if r == 0 else 0
        for k in (0, 1, 3, 2): umm(k)
        if r > 0:
            wrap(0, "TR", 0, S + TT, A("W0", 0, 76))
            wrap(0, "TR", S + TT, S + 2 * TT, A("W1", 0, 64))

        def side(p):
            o = 12 if p == 0 else 0
            if r > 0:
                cp(A("EL", 64 * p + 12 - o, 76 + 64 * p), A(WB[p], 0, o + 64))
                tt(A("DD", 64 * p, 64 * p + 64), A(WB[p], o, o + 64), A("TM", 0, 64), ALU.subtract)
                if p == 0: send(r)
            tt(A("V32", p * TT, (p + 1) * TT), W("F", 0, M + S, "EL", 12 + 64 * p, 76 + 64 * p), A("F2", p * TT, (p + 1) * TT), ALU.subtract)
        side(0); side(1)
        sql(0); sql(1); umm(4); umm(5); sql(2); sql(3)
        mm(A("K", 0, 256), I(1), A("TE", 0, 256), True, False)
        ssum("SL", 0, 0)
        if r > 0:
            q, lo, hi = TQ[-1]
            gat(q, A("TR", lo, hi), W("LR", 0, M + S, "EP", lo // 16, hi // 16))
            wrap(0, "TR", S + 2 * TT, S + M, A("W2", 0, 64))
            side(2)
        else:
            gat("S", A("MR", 0, TT), W("F", 0, M + S, "EL", 140, LW))
            for hf in range(2):
                o = A(UB[2 + hf], 0, 512)
                mm(o, I(1), A("MR", 512 * hf, 512 * hf + 512), True, False)
                mm(o, I(-1), A("F", 2 * TT + 512 * hf, 2 * TT + 512 * hf + 512), False, True)
            ts(A("TM", 0, 64), A("TI", 0, 64), J, ALU.add)
            ts(A("GS", 16, 32), A("GI", 0, 16), G16, ALU.is_equal, -1.0, ALU.mult)
            for k in range(RO): ms(A("CM", k * CW, k * CW + 16), -256.0)
            for p in range(3): tt(A("DD", 64 * p, 64 * p + 64), A("TW", 64 * p, 64 * p + 64), A("TM", 0, 64), ALU.subtract)
        sql(4); sql(5)
        ssum("SL", 1, 0)
        mm(KK(2), I(1), A("TE", 256, 384), True, False)
        ssum("SL", 2, 0)
        ts(A("BL", 0, 192), A("EL", 12, LW), float(16 - M), ALU.add, 0.0, ALU.max)
        ts(A("AN", 0, 192), A("DD", 0, 192), TT - 1, ALU.bitwise_and)
        if r > 0: ystep(r, 0)
        else: later()
        ts((T.IV[:, 0:384:2], ("IV", 0, 192)), A("AN", 0, 192), 0.0, ALU.is_equal)
        if r == 0:
            ts((T.IV[:, 1:384:2], ("IV", 192, 384)), A("AN", 0, 192), 0.0, ALU.is_equal)
            ystep(r, 0)
        else:
            add("G", lambda: g.affine_select(T.IV[:, 1:384:2], T.IV[:, 0:384:2], [[0, 192]], ALU.is_ge, 0.0, 0, 0), [("IV", 0, 192)], [("IV", 192, 384)])
        if r == 1: iota(A("LR32", 0, M + S), [[0, M + S]], 0, 0)
        for p in range(3 if r else 2): act(A("V32", p * TT, (p + 1) * TT), A("V32", p * TT, (p + 1) * TT), ACT.Square)
        if r == 0:
            for hf in range(2): act(A("V32", 2 * TT + 512 * hf, 2 * TT + 512 * hf + 512), A(UB[2 + hf], 0, 512), ACT.Square)
        ssum("V32", 0, 1); ssum("V32", 1, 1)
        inv(0); inv(1, True); inv(2)
        ssum("V32", 2, 1, True)
        ystep(r, 1)
        act(A("M0", 0, 128), KK(0), ACT.Relu)
        if r == 0: later_s()
        ystep(r, 2)
        tt(A("M1", 0, 128), KK(1), A("M0", 0, 128), ALU.max)
        tt(A("M2", 0, 128), KK(2), A("M1", 0, 128), ALU.max)
        for q in range(3): tt(A("ST", 128 * q, 128 * q + 128), KK(q), A("M2", 0, 128), ALU.is_ge)
        SD = [("U0", 0), ("U0", 256), ("U1", 0)]
        for b in ("U2", "U3"):
            for q in range(3): mm(A(b, 64 * q, 64 * q + 64), A("ST", 128 * q, 128 * q + 128), A("R4", 0, 64), True, True)
        for q in range(3): mm(A(SD[q][0], SD[q][1], SD[q][1] + 256), A("ST", 128 * q, 128 * q + 128), A("R4", 0, 256), True, True)
        wrap(1, "TR", 16 * c0, S + M, A("W0", c0, LW))
        act(A("SW", 0, 192), A("U3", 0, 192), ACT.Copy)
        ystep(r, 3)
        tt(A("PR", 0, 192), A("U2", 0, 192), A("DD", 0, 192), ALU.mult)
        tt(A("P1", 0, 64), A("PR", 0, 64), A("PR", 64, 128), ALU.add)
        tt(A("P2", 0, 64), A("PR", 128, 192), A("TM", 0, 64), ALU.add)
        Gi = A("Z", 0, 64)
        tt(Gi, A("P1", 0, 64), A("P2", 0, 64), ALU.add)
        ts(A("AI", 0, 64), Gi, 4, ALU.arith_shift_right)
        ts(A("BI", 0, 64), Gi, 15, ALU.bitwise_and)
        cp(A("MO", 0, 64), A("AI", 0, 64))
        ts(A("VAL", 64, 128), A("BI", 0, 64), J, ALU.subtract)
        gat("S", A("MR", MCUT, TT), W("SW", 0, 192, "MO", MCUT // 16, 64))
        if MCUT: gat("V", A("MR", 0, MCUT), W("SW", 0, 192, "MO", 0, MCUT // 16))
        act(A("PW", 0, 64), A("VAL", 64, 128), ACT.Exp, JL, -LN2)
        ts(A("N1", 0, 64), Gi, float(2 * TT), ALU.is_ge, float(-M), ALU.mult)
        tt(A("VAL", 0, 64), A("AI", 0, 64), A("AC", 0, 64), ALU.subtract)
        tt(A("N2", 0, 64), A("N1", 0, 64), Gi, ALU.add)
        ts(A("AT", 0, 64), A("AI", 0, 64), 64.0, ALU.is_ge, -192.0, ALU.mult)
        ts(A("NG", 0, 64), A("N2", 0, 64), float(TT), ALU.add)
        tt(A("VAL", 128, 192), A("AT", 0, 64), A("VAL", 0, 64), ALU.add)
        gat("S", A("NR", 0, TT), W("TR", S, S + M, "NG", 0, 64))
        mm(A("U2", 0, 64), I(1), A("HF", 0, 64), True, False)
        wrap(2, "MR", 0, TT, A("U2", 0, 64), False)
        act(A("TP", c0, LW), A("W0", c0, LW), ACT.Copy)
        ystep(r, 4)
        tt(A("X1", 0, 64), A("U2", 0, 64), A("PW", 0, 64), ALU.mult)
        cp(A("X2", 0, 64), A("X1", 0, 64))
        f = A("VF", 0, 64)
        tt(f, A("X2", 0, 64), A("X1", 0, 64), ALU.is_gt)
        for k in range(3): tt(A("VF", 64 * k + 64, 64 * k + 128), f, A("VAL", 64 * k, 64 * k + 64), ALU.mult)
        wrap(1, "NR", 0, TT, A("U3", 0, 64))
        for q in range(3): tt(A("MM", 256 * q, 256 * q + 256), A(SD[q][0], SD[q][1], SD[q][1] + 256), A("VF", 0, 256), ALU.mult)

        def mq(q, k):
            q %= 3
            return A("MM", 256 * q + 64 * k, 256 * q + 64 * k + 64)

        def asm(bank, base, terms):
            mm(*base, True, False)
            terms = [t for t in terms if t[1] != 0]
            for i, (c, w, s) in enumerate(terms): mm(A(bank, c, c + 64), I(w), s, False, i == len(terms) - 1)
        sc = 16 if last else 1
        terms = []
        for q in range(3):
            terms += [(64 * q, sc, mq(q - 1, 3)), (64 * q, sc * (128 - 64 * q), mq(q - 1, 0)), (64 * q, sc * (128, -64, -64)[q], mq(q + 1, 0)),
                      (64 * q + (0 if last else 192), 1, mq(q - 1, 2))]
        if last:
            asm("W1", (A("W1", 0, 192), I(16), A("AB", 0, 192)), terms)
            act(A("L32", 0, 192), A("W1", 0, 192), ACT.Identity, J)
            dma("Y", T.LR32[0:128:16, :], T.L32[:], [("L32", 0, LW)], [("LR32", 0, M + S)])
        else:
            asm("W1", (A("W1", 0, 384), I(1), A("AB", 0, 384)), terms)
            act(A("LA", 0, 192), A("W1", 0, 192), ACT.Copy)
            dma("Y", T.LR[0:128:16, :], T.LA[:], [("LA", 0, LW)], [("LR", 0, M + S - 1)])
            act(A("LB", 0, 192), A("W1", 192, 384), ACT.Copy)
            dma("Y", T.LR[1:128:16, :], T.LB[:], [("LB", 0, LW)], [("LR", M + S - 1, M + S)])
        terms = []
        for q in range(3):
            terms += [(64 * q, 16, mq(q, 3)), (64 * q, 2048 - TT * q, mq(q, 0)), (64 * q, 1, mq(q, 2)), (64 * q, 16, mq(q - 1, 1)),
                      (64 * q, -TT * q, mq(q - 1, 0)), (64 * q, 1, mq(q - 1, 2)), (64 * q, (TT, TT, -2 * TT)[q], mq(q + 1, 0))]
        asm("W2", (A("W2", 0, 192), I(16), A("AB", 0, 192)), terms)
        for q in range(3): tt(A("E1", 64 * q, 64 * q + 64), A("W0", 12 + 64 * q, 76 + 64 * q), mq(q - 1, 0), ALU.mult)
        for q in range(3): tt(A("E2", 64 * q, 64 * q + 64), A("W0", 12 + 64 * q, 76 + 64 * q), mq(q + 1, 0), ALU.mult)
        for q in range(3): tt(A("E3", 64 * q, 64 * q + 64), A("U3", 0, 64), mq(q + 1, 0), ALU.mult)
        mm(A("K", 0, LW), IP, A("TP", 0, LW), True, False)
        mm(A("K", 12, LW), IN, A("E1", 0, 192), False, False)
        mm(A("K", 12, LW), IN, A("E2", 0, 192), False, False)
        mm(A("K", 12, 140), IP, A("E2", 64, 192), False, False)
        mm(A("K", 140, LW), IP, A("E2", 0, 64), False, False)
        mm(A("K", 12, LW), IP, A("E3", 0, 192), False, True)
        ts(A("SR", 0, 192), A("W2", 0, 192), J, ALU.add)
        for q, p, hf in (FL if last else FQ):
            a = p * TT + hf * 512
            gat(q, A("F", a, a + 512), W("YF", 0, M, "SR", a // 16, a // 16 + 32))
            if hf == 1:
                a = p * TT; b = ((p + 2) % 3) * TT
                if last: dma("Y", T.yx[:, b:b + TT], T.F[:, a:a + TT], [("F", a, a + TT)], [])
                else: dma("Y", T.F2[:, a:a + TT], T.F[:, a:a + TT], [("F", a, a + TT)], [("F2", a, a + TT)])
        cp(A("EP", 0, LW), A("K", 0, LW))
        if last:
            for q, lo, hi in TL:
                gat(q, A("TW32", lo, hi), W("LR32", 0, M + S, "EP", 12 + lo // 16, 12 + hi // 16))
                dma("Y", T.yt[:, lo:hi], T.TW32[0:128:16, lo:hi], [("TW32", lo, hi)], [])
        else:
            for q, lo, hi in TQ[:-1]: gat(q, A("TR", lo, hi), W("LR", 0, M + S, "EP", lo // 16, hi // 16))
    return ops


def emit(g, T, ops):
    eng = {"V": g.vector, "S": g.scalar, "P": g.tensor, "G": g, "Y": g.sync}
    hist = {}; bank = {}; know = {q: {} for q in eng}; snap = []; waits = []; need = set()
    for i, (q, fn, rd, wr, kind) in enumerate(ops):
        deps = set()
        acc = [(x, False) for x in rd] + [(x, True) for x in wr]
        for (x, isw) in acc:
            for (j, lo, hi, w) in hist.get(x[0], []):
                if (w or isw) and lo < x[2] and x[1] < hi: deps.add(j)
            if x[0] in PSUM:
                for e, j in bank.get(x[0], {}).items():
                    if e != q: deps.add(j)
        mine = []
        if kind != "x":
            kn = know[q]
            for j in sorted(deps, reverse=True):
                qj, kj = ops[j][0], ops[j][4]
                if (qj == "P" and q == "P") or kj == "r": continue
                key = qj if kj == "c" else ("d", j)
                if kn.get(key, -1) >= j: continue
                mine.append(j); need.add(j); kn[key] = j
                for k2, v2 in snap[j].items():
                    if kn.get(k2, -1) < v2: kn[k2] = v2
            snap.append(dict(kn))
        else:
            snap.append({})
        waits.append(mine)
        for (x, isw) in acc:
            h = hist.setdefault(x[0], [])
            if isw: h[:] = [e for e in h if not (x[1] <= e[1] and e[2] <= x[2])]
            h.append((i, x[1], x[2], isw))
            if x[0] in PSUM: bank.setdefault(x[0], {})[q] = i
    cnt = {q: 0 for q in "VSPG"}; at = {}; nd = 0; sent = 0; dmas = []
    for i, (q, fn, rd, wr, kind) in enumerate(ops):
        if kind == "x":
            at[i] = fn
            continue
        for j in waits[i]: eng[q].wait_ge(T.sem[at[j][0]], at[j][1])
        ins = fn()
        if kind == "c" and i in need:
            cnt[q] += 1; ins.then_inc(T.sem["c" + q], 1); at[i] = ("c" + q, cnt[q])
        elif kind == "d":
            ins.then_inc(T.sem["d%d" % nd], 16); at[i] = ("d%d" % nd, 16); nd += 1
            if i not in need: dmas.append(at[i])
        elif kind == "r":
            sent += 8
    for s, v in dmas: g.sync.wait_ge(T.sem[s], v)
    g.wait_ge(T.sem.sent, sent)


def rank_program(g, core, T, topo):
    if T.rank_of(core) is None:
        return
    emit(g, T, build(g, core, T, topo))
